import numpy as np
import ml_dtypes


def mxq(x, axis, fmt="e4m3"):
    dtype, down = {"e4m3": (ml_dtypes.float8_e4m3fn, 7), "e5m2": (ml_dtypes.float8_e5m2, 14)}[fmt]
    v = np.moveaxis(np.asarray(x, np.float32).astype(ml_dtypes.bfloat16).astype(np.float64), axis, -1)
    blocks = v.reshape(v.shape[:-1] + (-1, 32))
    amax = np.abs(blocks).max(-1, keepdims=True)
    byte = np.maximum(np.where(amax > 0, np.frexp(amax)[1] - 1 + 127, 0) - down, 1)
    scale = np.exp2(byte - 127.0)
    codes = (blocks / scale).astype(np.float32).astype(dtype).astype(np.float64)
    return np.moveaxis((codes * scale).reshape(v.shape), -1, axis)


WIDE = False


def mx_kscale(k):
    if not WIDE:
        return np.ones(k)
    levels = np.array([10, -10, 5, -5, 0])
    if k % 512:
        return np.exp2(np.random.permutation(np.resize(levels, k // 32))).repeat(32)
    a = np.empty((k // 512, 16))
    for p in range(k // 512):
        a[p, :8] = np.random.permutation(np.resize(levels, 8))
        for g in range(8):
            far = levels[np.abs(levels - a[p, g]) >= 10]
            a[p, g + 8] = far[np.random.randint(len(far))]
    return np.exp2(a.ravel()).repeat(32)


def f64(x):
    return np.asarray(x).astype(np.float64)


def striped(idx):
    return np.tile(idx.reshape(-1, 16).T, (8, 1)).astype(np.uint16)


def unstriped(offs):
    return offs[:16].T.reshape(-1).astype(np.int64)


def pack_weight(w):
    k, n = w.shape
    w = f64(np.asarray(w, np.float32).astype(ml_dtypes.bfloat16)).reshape(k // 32, 32, n)
    amax = np.abs(w).max(1)
    byte = np.clip(np.where(amax > 0, np.frexp(amax)[1] - 1 + 127 - 7, 1), 1, 254)
    scaled = (w * np.exp2(127.0 - byte)[:, None, :]).reshape(k, n).astype(np.float32)
    words = np.ascontiguousarray(scaled.reshape(k // 512, 128, 4, n).transpose(0, 1, 3, 2)).astype(ml_dtypes.float8_e4m3fn).view(np.uint8)
    return words, np.ascontiguousarray(byte.astype(np.uint8).reshape(k // 512, 16, n))


def unpack_weight(words, scales):
    g, p, n, _ = words.shape
    vals = np.ascontiguousarray(words).view(ml_dtypes.float8_e4m3fn).astype(np.float64) * np.repeat(np.exp2(scales.astype(np.float64) - 127.0), 8, axis=1)[..., None]
    return vals.transpose(0, 1, 3, 2).reshape(g * 512, n)


K, T, S, N, H, W, G, U = 512, 1024, 512, 256, 512, 1024, 1024, 1024


def setup_inputs():
    n = np.random.standard_normal
    s = mx_kscale(K)[:, None]
    u = mx_kscale(H)
    packed_xT = pack_weight(n((K, T)) * s)
    packed_eT = pack_weight(n((K, W)) * s)
    packed_dT = pack_weight(n((K, G)) * s)
    return {
        "x_words": packed_xT[0],
        "x_scales": packed_xT[1],
        "w1": (n((K, H)) / np.sqrt(K) / s).astype(np.float32),
        "e_words": packed_eT[0],
        "e_scales": packed_eT[1],
        "w2": (n((K, H)) / np.sqrt(K) / s).astype(np.float32),
        "d_words": packed_dT[0],
        "d_scales": packed_dT[1],
        "w3": (n((K, H)) / np.sqrt(K) / s).astype(np.float32),
        "unit": (np.random.uniform(0.6, 1.4, (H, 1)) * u[:, None]).astype(np.float32),
        "w4": (n((H, N)) / np.sqrt(H) / u[:, None]).astype(np.float32),
        "offs": striped(np.random.permutation(T)[:S]),
        "prd": striped(np.random.permutation(W)[:S]),
        "shp": striped(np.random.permutation(G)[:S]),
        "fk": striped(np.random.permutation(np.concatenate([np.arange(S), np.random.randint(0, S, U - S)]))),
        "dk1": striped(np.random.permutation(np.concatenate([np.arange(S), np.random.randint(0, S, U - S)]))),
        "dk2": striped(np.random.permutation(np.concatenate([np.arange(S), np.random.randint(0, S, U - S)]))),
    }


def reference(x_words, x_scales, w1, e_words, e_scales, w2, d_words, d_scales, w3, unit, w4, offs, prd, shp, fk, dk1, dk2):
    xq = unpack_weight(x_words, x_scales)[:, unstriped(offs)]
    y = mxq(f64(w1), 0, "e4m3").T @ xq
    ff = y[:, unstriped(fk)]
    e_prd = unpack_weight(e_words, e_scales)[:, unstriped(prd)]
    ye = mxq(f64(w2), 0, "e4m3").T @ e_prd
    pp1 = ye[:, unstriped(dk1)]
    d_shp = unpack_weight(d_words, d_scales)[:, unstriped(shp)]
    yd = mxq(f64(w3), 0, "e4m3").T @ d_shp
    ss1 = yd[:, unstriped(dk2)]
    join = ff * pp1 + 0.7 * ss1
    hid = f64(unit) * join
    return mxq(f64(w4), 0, "e4m3").T @ mxq(hid, 0, "e4m3")

@@ -1,0 +1,198 @@
+from contextlib import ExitStack
+
+import concourse.mybir as mybir
+
+F32 = mybir.dt.float32
+BF16 = mybir.dt.bfloat16
+I32 = mybir.dt.int32
+U32 = mybir.dt.uint32
+U16 = mybir.dt.uint16
+U8 = mybir.dt.uint8
+FP8X4 = mybir.dt.float8_e4m3fn_x4
+MULT = mybir.AluOpType.mult
+ADD = mybir.AluOpType.add
+COPY = mybir.ActivationFunctionType.Copy
+
+P = 128
+PACK = 4
+K, T, S, H, N, U = 512, 1024, 512, 512, 256, 1024
+CHUNKS = (256,256,256,256)
+SHOP_ON_VECTOR = (2,0,0,0)
+OUT_ON_SCALAR = (0,0,0,1)
+FLOPS = 2 * K * H * S * 3 + 2 * H * N * U
+
+
+def tile_picked_ystarjn_sum_p_kernel(
+    tc, x_words, x_scales, w1, e_words, e_scales, w2, d_words, d_scales, w3, unit, w4,
+    offs, prd, shp, fk, dk1, dk2, out,
+):
+    nc = tc.nc
+    with ExitStack() as ctx:
+        keep = ctx.enter_context(tc.tile_pool(name="keep", bufs=1))
+        ring = ctx.enter_context(tc.tile_pool(name="ring", bufs=2))
+        banks = ctx.enter_context(tc.psum_pool(name="banks", bufs=6))
+        out_banks = ctx.enter_context(tc.psum_pool(name="out_banks", bufs=2))
+
+        def load_list(src, name):
+            tile = keep.tile(list(src.shape), U16, name=name)
+            nc.sync.dma_start(tile[:], src)
+            return tile
+
+        def load_scales(src, name, clearer, queue):
+            tile = keep.tile([P, T], U8, name=name, align_bytes=64)
+            clearer.memset(tile[:].bitcast(I32), 0)
+            for r in range(4):
+                queue.dma_start(tile[r:P:32, :].bitcast(I32), src[0, r:16:4, :].bitcast(I32))
+            return tile
+
+        def load_words(src, name):
+            tile = keep.tile([P, T], U32, name=name, align_bytes=64)
+            nc.sync.dma_start(tile[:].bitcast(I32), src[0].rearrange("p c r -> p (c r)").bitcast(I32))
+            return tile
+
+        def load_weight(src, name):
+            tile = keep.tile([P, PACK, src.shape[1]], F32, name=name, tag=name)
+            nc.sync.dma_start(tile[:], src.rearrange("(p j) c -> p j c", j=PACK))
+            return tile
+
+        def pick(words, scales, picks, name):
+            got_words = keep.tile([P, S], U32, name=name + "_words_picked", align_bytes=64)
+            nc.vector.tensor_copy(got_words[:], words[:].indirect(picks[:]))
+            got_scales = keep.tile([P, S], U8, name=name + "_scales_picked", align_bytes=64)
+            nc.vector.tensor_copy(got_scales[:], scales[:].indirect(picks[:]))
+            return got_words, got_scales
+
+        def quantize(rounded, width, name):
+            codes = keep.tile([P, width], U32, name=name + "_codes", align_bytes=64)
+            scales = keep.tile([P, width], U8, name=name + "_scales", align_bytes=64)
+            nc.vector.quantize_mx(out=codes[:].bitcast(FP8X4), scales=scales[:], in_=rounded)
+            return codes, scales
+
+        def round_dealt(parts, name):
+            rounded = keep.tile([P, PACK, P, PACK], BF16, name=name + "_bf16", tag=name + "_bf16", align_bytes=64)
+            dst = rounded[:].rearrange("p t m j -> p m j t")
+            m0 = 0
+            for raw, on_scalar in parts:
+                src = raw[:].rearrange("p j (m t) -> p m j t", t=PACK)
+                width = src.shape[1]
+                if on_scalar > 0:
+                    nc.scalar.activation(dst[:, m0:m0 + on_scalar], src[:, :on_scalar], COPY)
+                if on_scalar < width:
+                    nc.vector.tensor_copy(dst[:, m0 + on_scalar:m0 + width], src[:, on_scalar:])
+                m0 = m0 + width
+            return rounded[:].rearrange("p t m j -> p (t m j)")
+
+        def product(w_codes, w_scales, got_words, got_scales, factor, name):
+            rows = []
+            for t in range(PACK):
+                bank = banks.tile([P, S], F32, name="bank")
+                cols = slice(t * P, (t + 1) * P)
+                nc.tensor.matmul_mx(
+                    out=bank[:], lhsT=w_codes[:, cols].bitcast(FP8X4), lhsT_scale=w_scales[:, cols],
+                    rhs=got_words[:].bitcast(FP8X4), rhs_scale=got_scales[:], start=True, stop=True,
+                )
+                row = keep.tile([P, S], F32, name=name + str(t))
+                if factor is None:
+                    nc.scalar.copy(row[:], bank[:])
+                else:
+                    nc.scalar.activation(row[:], bank[:], COPY, scale=factor[:, t:t + 1])
+                rows.append(row)
+            return rows
+
+        x_word_rows = load_words(x_words, "x_word_rows")
+        offs_sb = load_list(offs, "offs_sb")
+        x_scale_rows = load_scales(x_scales, "x_scale_rows", nc.vector, nc.sync)
+        w1_low = load_weight(w1[:, :H // 2], "w1_low")
+        w1_high = load_weight(w1[:, H // 2:], "w1_high")
+        unit_sb = keep.tile([P, PACK], F32, name="unit_sb")
+        nc.sync.dma_start(unit_sb[:], unit.rearrange("(p t) o -> p (t o)", t=PACK))
+        e_word_rows = load_words(e_words, "e_word_rows")
+        fk_sb = load_list(fk, "fk_sb")
+        prd_sb = load_list(prd, "prd_sb")
+        e_scale_rows = load_scales(e_scales, "e_scale_rows", nc.vector, nc.sync)
+        d_word_rows = load_words(d_words, "d_word_rows")
+        shp_sb = load_list(shp, "shp_sb")
+        d_scale_rows = load_scales(d_scales, "d_scale_rows", nc.vector, nc.sync)
+        w2_raw = load_weight(w2, "w2_raw")
+        dk1_sb = load_list(dk1, "dk1_sb")
+        w3_raw = load_weight(w3, "w3_raw")
+        dk2_sb = load_list(dk2, "dk2_sb")
+        w4_raw = load_weight(w4, "w4_raw")
+
+        shop_unit = keep.tile([P, PACK], F32, name="shop_unit")
+
+        x_got = pick(x_word_rows, x_scale_rows, offs_sb, "x")
+        w1_q = quantize(round_dealt([(w1_low, 64), (w1_high, 24)], "w1"), H, "w1")
+        nc.vector.tensor_scalar(shop_unit[:], unit_sb[:], 0.7, None, MULT)
+        fact = product(*w1_q, *x_got, unit_sb, "fact")
+        e_got = pick(e_word_rows, e_scale_rows, prd_sb, "e")
+        d_got = pick(d_word_rows, d_scale_rows, shp_sb, "d")
+        w2_q = quantize(round_dealt([(w2_raw, 0)], "w2"), H, "w2")
+        goods = product(*w2_q, *e_got, None, "goods")
+        w3_q = quantize(round_dealt([(w3_raw, 0)], "w3"), H, "w3")
+        shop = product(*w3_q, *d_got, shop_unit, "shop")
+
+        w4_bf16 = keep.tile([P, N, PACK], BF16, name="w4_bf16", align_bytes=64)
+        nc.vector.tensor_copy(
+            w4_bf16[:].rearrange("p (c i) j -> p c j i", i=4), w4_raw[:].rearrange("p j (c i) -> p c j i", i=4))
+        w4_codes, w4_scales = quantize(w4_bf16[:].rearrange("p c j -> p (c j)"), N, "w4")
+
+        starts = [sum(CHUNKS[:c]) for c in range(len(CHUNKS))]
+        fact_parts, joined_parts, shop_parts = {}, {}, {}
+
+        def entries(c):
+            return slice(starts[c] // 16, (starts[c] + CHUNKS[c]) // 16)
+
+        def fetch_facts(c):
+            fact_parts[c] = keep.tile(
+                [P, PACK, CHUNKS[c]], F32, name="fact_part", tag=("w1_bf16", "fact_spare", "w3_bf16")[c % 3], align_bytes=64)
+            for t in range(PACK):
+                nc.scalar.activation(fact_parts[c][:, t, :], fact[t][:].indirect(fk_sb[:, entries(c)]), COPY)
+
+        def times_goods(c):
+            joined_parts[c] = keep.tile([P, PACK, CHUNKS[c]], F32, name="joined", tag=("w3_raw", "w4_raw")[c % 2])
+            for t in range(PACK):
+                nc.vector.tensor_tensor(
+                    joined_parts[c][:, t, :], goods[t][:].indirect(dk1_sb[:, entries(c)]), fact_parts[c][:, t, :], MULT)
+
+        def fetch_shops(c):
+            shop_parts[c] = ring.tile([P, PACK, CHUNKS[c]], F32, name="shop_part")
+            for t in range(PACK):
+                if t < SHOP_ON_VECTOR[c]:
+                    nc.vector.tensor_copy(shop_parts[c][:, t, :], shop[t][:].indirect(dk2_sb[:, entries(c)]))
+                else:
+                    nc.scalar.activation(shop_parts[c][:, t, :], shop[t][:].indirect(dk2_sb[:, entries(c)]), COPY)
+
+        def finish(c):
+            n = CHUNKS[c]
+            hid = ring.tile([P, n, PACK], BF16, name="hid", align_bytes=64)
+            nc.vector.tensor_tensor(
+                hid[:].rearrange("p (c i) t -> p c t i", i=4),
+                joined_parts[c][:].rearrange("p t (c i) -> p c t i", i=4),
+                shop_parts[c][:].rearrange("p t (c i) -> p c t i", i=4), ADD)
+            hid_codes, hid_scales = quantize(hid[:].rearrange("p r t -> p (r t)"), n, "hid" + str(c))
+            acc = out_banks.tile([P, N // P, n], F32, name="acc")
+            for b in range(N // P):
+                cols = slice(b * P, (b + 1) * P)
+                nc.tensor.matmul_mx(
+                    out=acc[:, b, :], lhsT=w4_codes[:, cols].bitcast(FP8X4), lhsT_scale=w4_scales[:, cols],
+                    rhs=hid_codes[:].bitcast(FP8X4), rhs_scale=hid_scales[:], start=True, stop=True,
+                )
+            result = ring.tile([P, N // P, n], F32, name="result")
+            if OUT_ON_SCALAR[c]:
+                nc.scalar.copy(result[:], acc[:])
+            else:
+                nc.vector.tensor_copy(result[:], acc[:])
+            nc.sync.dma_start(out[:, starts[c]:starts[c] + n].rearrange("(b p) r -> p b r", p=P), result[:])
+
+        last = len(CHUNKS) - 1
+        fetch_facts(0)
+        fetch_facts(1)
+        times_goods(0)
+        for c in range(len(CHUNKS)):
+            fetch_shops(c)
+            if c + 2 <= last:
+                fetch_facts(c + 2)
+            if c + 1 <= last:
+                times_goods(c + 1)
+            finish(c)

@@ -16,9 +16,14 @@ COPY = mybir.ActivationFunctionType.Copy
 P = 128
 PACK = 4
 K, T, S, H, N, U = 512, 1024, 512, 512, 256, 1024
-CHUNKS = (256,256,256,256)
-SHOP_ON_VECTOR = (2,0,0,0)
-OUT_ON_SCALAR = (0,0,0,1)
+CHUNKS = (256,256,256,128,128)
+SHOP_ON_VECTOR = (1,1,0,0,0)
+OUT_ON_SCALAR = (0,1,1,1,2)
+PIECES = (256,256,256,128,128)
+FACT_TAGS = ("w1_bf16", "fact_spare", "w3_bf16", "w1_bf16", "fact_spare")
+JOIN_TAGS = ("w3_raw", "w4_raw", "w3_raw", "w4_raw", "w3_raw")
+FACT_ON_VECTOR = (0,0,0,0,0,0)
+FUSED = (0,0,0,0,0,0)
 FLOPS = 2 * K * H * S * 3 + 2 * H * N * U
 
 
@@ -29,9 +34,9 @@ def tile_picked_ystarjn_sum_p_kernel(
     nc = tc.nc
     with ExitStack() as ctx:
         keep = ctx.enter_context(tc.tile_pool(name="keep", bufs=1))
-        ring = ctx.enter_context(tc.tile_pool(name="ring", bufs=2))
-        banks = ctx.enter_context(tc.psum_pool(name="banks", bufs=6))
-        out_banks = ctx.enter_context(tc.psum_pool(name="out_banks", bufs=2))
+        ring = ctx.enter_context(tc.tile_pool(name="ring", bufs=3))
+        banks = ctx.enter_context(tc.psum_pool(name="banks", bufs=4))
+        out_banks = ctx.enter_context(tc.psum_pool(name="out_banks", bufs=4))
 
         def load_list(src, name):
             tile = keep.tile(list(src.shape), U16, name=name)
@@ -68,17 +73,28 @@ def tile_picked_ystarjn_sum_p_kernel(
             nc.vector.quantize_mx(out=codes[:].bitcast(FP8X4), scales=scales[:], in_=rounded)
             return codes, scales
 
+        def quantize_planes(rounded, width, name):
+            codes = keep.tile([P, width], U32, name=name + "_codes", align_bytes=64)
+            scales = keep.tile([P, width], U8, name=name + "_scales", align_bytes=64)
+            for a, b in ((0, 128), (128, 512)):
+                nc.vector.quantize_mx(
+                    out=codes[:, a:b].bitcast(FP8X4), scales=scales[:, a:b], in_=rounded[:, PACK * a:PACK * b])
+            return codes, scales
+
         def round_dealt(parts, name):
             rounded = keep.tile([P, PACK, P, PACK], BF16, name=name + "_bf16", tag=name + "_bf16", align_bytes=64)
             dst = rounded[:].rearrange("p t m j -> p m j t")
             m0 = 0
-            for raw, on_scalar in parts:
+            for raw, on_scalar, on_gpsimd in parts:
                 src = raw[:].rearrange("p j (m t) -> p m j t", t=PACK)
                 width = src.shape[1]
                 if on_scalar > 0:
                     nc.scalar.activation(dst[:, m0:m0 + on_scalar], src[:, :on_scalar], COPY)
-                if on_scalar < width:
-                    nc.vector.tensor_copy(dst[:, m0 + on_scalar:m0 + width], src[:, on_scalar:])
+                rest = width - on_gpsimd
+                if on_scalar < rest:
+                    nc.vector.tensor_copy(dst[:, m0 + on_scalar:m0 + rest], src[:, on_scalar:rest])
+                if on_gpsimd > 0:
+                    nc.gpsimd.tensor_scalar(dst[:, m0 + rest:m0 + width], src[:, rest:], 1.0, 0.0, MULT, ADD)
                 m0 = m0 + width
             return rounded[:].rearrange("p t m j -> p (t m j)")
 
@@ -122,14 +138,14 @@ def tile_picked_ystarjn_sum_p_kernel(
         shop_unit = keep.tile([P, PACK], F32, name="shop_unit")
 
         x_got = pick(x_word_rows, x_scale_rows, offs_sb, "x")
-        w1_q = quantize(round_dealt([(w1_low, 64), (w1_high, 24)], "w1"), H, "w1")
+        w1_q = quantize_planes(round_dealt([(w1_low, 64, 0), (w1_high, 24, 0)], "w1"), H, "w1")
         nc.vector.tensor_scalar(shop_unit[:], unit_sb[:], 0.7, None, MULT)
         fact = product(*w1_q, *x_got, unit_sb, "fact")
         e_got = pick(e_word_rows, e_scale_rows, prd_sb, "e")
         d_got = pick(d_word_rows, d_scale_rows, shp_sb, "d")
-        w2_q = quantize(round_dealt([(w2_raw, 0)], "w2"), H, "w2")
+        w2_q = quantize(round_dealt([(w2_raw, 0, 0)], "w2"), H, "w2")
         goods = product(*w2_q, *e_got, None, "goods")
-        w3_q = quantize(round_dealt([(w3_raw, 0)], "w3"), H, "w3")
+        w3_q = quantize(round_dealt([(w3_raw, 0, 0)], "w3"), H, "w3")
         shop = product(*w3_q, *d_got, shop_unit, "shop")
 
         w4_bf16 = keep.tile([P, N, PACK], BF16, name="w4_bf16", align_bytes=64)
@@ -138,39 +154,77 @@ def tile_picked_ystarjn_sum_p_kernel(
         w4_codes, w4_scales = quantize(w4_bf16[:].rearrange("p c j -> p (c j)"), N, "w4")
 
         starts = [sum(CHUNKS[:c]) for c in range(len(CHUNKS))]
+        piece_starts = [sum(PIECES[:c]) for c in range(len(PIECES))]
         fact_parts, joined_parts, shop_parts = {}, {}, {}
 
-        def entries(c):
-            return slice(starts[c] // 16, (starts[c] + CHUNKS[c]) // 16)
+        def entries(start, n):
+            return slice(start // 16, (start + n) // 16)
 
-        def fetch_facts(c):
-            fact_parts[c] = keep.tile(
-                [P, PACK, CHUNKS[c]], F32, name="fact_part", tag=("w1_bf16", "fact_spare", "w3_bf16")[c % 3], align_bytes=64)
-            for t in range(PACK):
-                nc.scalar.activation(fact_parts[c][:, t, :], fact[t][:].indirect(fk_sb[:, entries(c)]), COPY)
+        def fetch_facts(h, planes):
+            if h not in fact_parts:
+                fact_parts[h] = keep.tile(
+                    [P, PACK, PIECES[h]], F32, name="fact_part", tag=FACT_TAGS[h], align_bytes=64)
+            for t in planes:
+                picked = fact[t][:].indirect(fk_sb[:, entries(piece_starts[h], PIECES[h])])
+                if t >= PACK - FACT_ON_VECTOR[h]:
+                    nc.vector.tensor_copy(fact_parts[h][:, t, :], picked)
+                else:
+                    nc.scalar.activation(fact_parts[h][:, t, :], picked, COPY)
 
-        def times_goods(c):
-            joined_parts[c] = keep.tile([P, PACK, CHUNKS[c]], F32, name="joined", tag=("w3_raw", "w4_raw")[c % 2])
-            for t in range(PACK):
+        def times_goods(h, planes):
+            if h not in joined_parts:
+                joined_parts[h] = keep.tile([P, PACK, PIECES[h]], F32, name="joined", tag=JOIN_TAGS[h])
+            for t in planes:
                 nc.vector.tensor_tensor(
-                    joined_parts[c][:, t, :], goods[t][:].indirect(dk1_sb[:, entries(c)]), fact_parts[c][:, t, :], MULT)
+                    joined_parts[h][:, t, :], goods[t][:].indirect(dk1_sb[:, entries(piece_starts[h], PIECES[h])]),
+                    fact_parts[h][:, t, :], MULT)
 
         def fetch_shops(c):
             shop_parts[c] = ring.tile([P, PACK, CHUNKS[c]], F32, name="shop_part")
+            h = max(k for k in range(len(PIECES)) if piece_starts[k] <= starts[c])
+            inside = starts[c] - piece_starts[h]
             for t in range(PACK):
-                if t < SHOP_ON_VECTOR[c]:
-                    nc.vector.tensor_copy(shop_parts[c][:, t, :], shop[t][:].indirect(dk2_sb[:, entries(c)]))
+                picked = shop[t][:].indirect(dk2_sb[:, entries(starts[c], CHUNKS[c])])
+                if FUSED[c]:
+                    nc.vector.tensor_tensor(
+                        shop_parts[c][:, t, :], picked, joined_parts[h][:, t, inside:inside + CHUNKS[c]], ADD)
+                elif t < SHOP_ON_VECTOR[c]:
+                    nc.vector.tensor_copy(shop_parts[c][:, t, :], picked)
                 else:
-                    nc.scalar.activation(shop_parts[c][:, t, :], shop[t][:].indirect(dk2_sb[:, entries(c)]), COPY)
+                    nc.scalar.activation(shop_parts[c][:, t, :], picked, COPY)
 
         def finish(c):
             n = CHUNKS[c]
+            h = max(k for k in range(len(PIECES)) if piece_starts[k] <= starts[c])
+            inside = starts[c] - piece_starts[h]
             hid = ring.tile([P, n, PACK], BF16, name="hid", align_bytes=64)
-            nc.vector.tensor_tensor(
-                hid[:].rearrange("p (c i) t -> p c t i", i=4),
-                joined_parts[c][:].rearrange("p t (c i) -> p c t i", i=4),
-                shop_parts[c][:].rearrange("p t (c i) -> p c t i", i=4), ADD)
+            woven = hid[:].rearrange("p (c i) t -> p c t i", i=4)
+            shop_woven = shop_parts[c][:].rearrange("p t (c i) -> p c t i", i=4)
+            if FUSED[c] == 1:
+                nc.vector.tensor_copy(woven, shop_woven)
+            elif FUSED[c] == 2:
+                nc.scalar.copy(woven, shop_woven)
+            else:
+                nc.vector.tensor_tensor(
+                    woven, joined_parts[h][:, :, inside:inside + n].rearrange("p t (c i) -> p c t i", i=4), shop_woven, ADD)
             hid_codes, hid_scales = quantize(hid[:].rearrange("p r t -> p (r t)"), n, "hid" + str(c))
+            cols_out = slice(starts[c], starts[c] + n)
+            if OUT_ON_SCALAR[c] == 2:
+                for b in range(N // P):
+                    cols = slice(b * P, (b + 1) * P)
+                    acc = out_banks.tile([P, n], F32, name="acc")
+                    nc.tensor.matmul_mx(
+                        out=acc[:], lhsT=w4_codes[:, cols].bitcast(FP8X4), lhsT_scale=w4_scales[:, cols],
+                        rhs=hid_codes[:].bitcast(FP8X4), rhs_scale=hid_scales[:], start=True, stop=True,
+                    )
+                    result = ring.tile([P, n], F32, name="last_result")
+                    if b == 0:
+                        nc.scalar.copy(result[:], acc[:])
+                        nc.scalar.dma_start(out[cols, cols_out], result[:])
+                    else:
+                        nc.vector.tensor_copy(result[:], acc[:])
+                        nc.sync.dma_start(out[cols, cols_out], result[:])
+                return
             acc = out_banks.tile([P, N // P, n], F32, name="acc")
             for b in range(N // P):
                 cols = slice(b * P, (b + 1) * P)
@@ -183,16 +237,25 @@ def tile_picked_ystarjn_sum_p_kernel(
                 nc.scalar.copy(result[:], acc[:])
             else:
                 nc.vector.tensor_copy(result[:], acc[:])
-            nc.sync.dma_start(out[:, starts[c]:starts[c] + n].rearrange("(b p) r -> p b r", p=P), result[:])
+            nc.sync.dma_start(out[:, cols_out].rearrange("(b p) r -> p b r", p=P), result[:])
 
-        last = len(CHUNKS) - 1
-        fetch_facts(0)
-        fetch_facts(1)
-        times_goods(0)
-        for c in range(len(CHUNKS)):
-            fetch_shops(c)
-            if c + 2 <= last:
-                fetch_facts(c + 2)
-            if c + 1 <= last:
-                times_goods(c + 1)
-            finish(c)
+        fetch_facts(0, [0,1,2,3])
+        fetch_facts(1, [0,1,2,3])
+        times_goods(0, [0,1,2,3])
+        fetch_shops(0)
+        fetch_facts(2, [0,1,2,3])
+        times_goods(1, [0,1,2,3])
+        finish(0)
+        fetch_shops(1)
+        fetch_facts(3, [0,1,2,3])
+        times_goods(2, [0,1,2,3])
+        finish(1)
+        fetch_shops(2)
+        fetch_facts(4, [0,1,2,3])
+        times_goods(3, [0,1,2,3])
+        finish(2)
+        fetch_shops(3)
+        times_goods(4, [0,1,2,3])
+        finish(3)
+        fetch_shops(4)
+        finish(4)

@@ -17,9 +17,9 @@ P = 128
 PACK = 4
 K, T, S, H, N, U = 512, 1024, 512, 512, 256, 1024
 CHUNKS = (256,256,256,128,128)
-SHOP_ON_VECTOR = (1,1,0,0,0)
-OUT_ON_SCALAR = (0,1,1,1,2)
-PIECES = (256,256,256,128,128)
+SHOP_ON_VECTOR = (1,0,0,0,0)
+OUT_ON_SCALAR = (1,1,1,1,2)
+PIECES = (256, 256, 256, 256)
 FACT_TAGS = ("w1_bf16", "fact_spare", "w3_bf16", "w1_bf16", "fact_spare")
 JOIN_TAGS = ("w3_raw", "w4_raw", "w3_raw", "w4_raw", "w3_raw")
 FACT_ON_VECTOR = (0,0,0,0,0,0)
@@ -83,16 +83,17 @@ def tile_picked_ystarjn_sum_p_kernel(
 
         def round_dealt(parts, name):
             rounded = keep.tile([P, PACK, P, PACK], BF16, name=name + "_bf16", tag=name + "_bf16", align_bytes=64)
-            dst = rounded[:].rearrange("p t m j -> p m j t")
+            dst = rounded[:].rearrange("p (a b) m j -> p a m j b", a=2)
             m0 = 0
             for raw, on_scalar, on_gpsimd in parts:
-                src = raw[:].rearrange("p j (m t) -> p m j t", t=PACK)
-                width = src.shape[1]
+                src = raw[:].rearrange("p j (m a b) -> p a m j b", a=2, b=2)
+                width = src.shape[2]
                 if on_scalar > 0:
-                    nc.scalar.activation(dst[:, m0:m0 + on_scalar], src[:, :on_scalar], COPY)
+                    for a in range(2):
+                        nc.scalar.activation(dst[:, a, m0:m0 + on_scalar], src[:, a, :on_scalar], COPY)
                 rest = width - on_gpsimd
                 if on_scalar < rest:
-                    nc.vector.tensor_copy(dst[:, m0 + on_scalar:m0 + rest], src[:, on_scalar:rest])
+                    nc.vector.tensor_copy(dst[:, :, m0 + on_scalar:m0 + rest], src[:, :, on_scalar:rest])
                 if on_gpsimd > 0:
                     nc.gpsimd.tensor_scalar(dst[:, m0 + rest:m0 + width], src[:, rest:], 1.0, 0.0, MULT, ADD)
                 m0 = m0 + width
@@ -137,9 +138,9 @@ def tile_picked_ystarjn_sum_p_kernel(
 
         shop_unit = keep.tile([P, PACK], F32, name="shop_unit")
 
+        nc.scalar.activation(shop_unit[:], unit_sb[:], COPY, scale=0.7)
         x_got = pick(x_word_rows, x_scale_rows, offs_sb, "x")
         w1_q = quantize_planes(round_dealt([(w1_low, 64, 0), (w1_high, 24, 0)], "w1"), H, "w1")
-        nc.vector.tensor_scalar(shop_unit[:], unit_sb[:], 0.7, None, MULT)
         fact = product(*w1_q, *x_got, unit_sb, "fact")
         e_got = pick(e_word_rows, e_scale_rows, prd_sb, "e")
         d_got = pick(d_word_rows, d_scale_rows, shp_sb, "d")
@@ -150,7 +151,7 @@ def tile_picked_ystarjn_sum_p_kernel(
 
         w4_bf16 = keep.tile([P, N, PACK], BF16, name="w4_bf16", align_bytes=64)
         nc.vector.tensor_copy(
-            w4_bf16[:].rearrange("p (c i) j -> p c j i", i=4), w4_raw[:].rearrange("p j (c i) -> p c j i", i=4))
+            w4_bf16[:].rearrange("p (c i) j -> p c j i", i=2), w4_raw[:].rearrange("p j (c i) -> p c j i", i=2))
         w4_codes, w4_scales = quantize(w4_bf16[:].rearrange("p c j -> p (c j)"), N, "w4")
 
         starts = [sum(CHUNKS[:c]) for c in range(len(CHUNKS))]
@@ -198,15 +199,15 @@ def tile_picked_ystarjn_sum_p_kernel(
             h = max(k for k in range(len(PIECES)) if piece_starts[k] <= starts[c])
             inside = starts[c] - piece_starts[h]
             hid = ring.tile([P, n, PACK], BF16, name="hid", align_bytes=64)
-            woven = hid[:].rearrange("p (c i) t -> p c t i", i=4)
-            shop_woven = shop_parts[c][:].rearrange("p t (c i) -> p c t i", i=4)
+            woven = hid[:].rearrange("p (c i) t -> p c t i", i=2)
+            shop_woven = shop_parts[c][:].rearrange("p t (c i) -> p c t i", i=2)
             if FUSED[c] == 1:
                 nc.vector.tensor_copy(woven, shop_woven)
             elif FUSED[c] == 2:
                 nc.scalar.copy(woven, shop_woven)
             else:
                 nc.vector.tensor_tensor(
-                    woven, joined_parts[h][:, :, inside:inside + n].rearrange("p t (c i) -> p c t i", i=4), shop_woven, ADD)
+                    woven, joined_parts[h][:, :, inside:inside + n].rearrange("p t (c i) -> p c t i", i=2), shop_woven, ADD)
             hid_codes, hid_scales = quantize(hid[:].rearrange("p r t -> p (r t)"), n, "hid" + str(c))
             cols_out = slice(starts[c], starts[c] + n)
             if OUT_ON_SCALAR[c] == 2:
@@ -251,11 +252,9 @@ def tile_picked_ystarjn_sum_p_kernel(
         times_goods(2, [0,1,2,3])
         finish(1)
         fetch_shops(2)
-        fetch_facts(4, [0,1,2,3])
         times_goods(3, [0,1,2,3])
         finish(2)
         fetch_shops(3)
-        times_goods(4, [0,1,2,3])
-        finish(3)
         fetch_shops(4)
+        finish(3)
         finish(4)

@@ -15,16 +15,19 @@ COPY = mybir.ActivationFunctionType.Copy
 
 P = 128
 PACK = 4
+LIST_ROWS = 16
+BLOCK = 32
+QUADRANT = 32
 K, T, S, H, N, U = 512, 1024, 512, 512, 256, 1024
-CHUNKS = (256,256,256,128,128)
-SHOP_ON_VECTOR = (1,0,0,0,0)
-OUT_ON_SCALAR = (1,1,1,1,2)
-PIECES = (256, 256, 256, 256)
-FACT_TAGS = ("w1_bf16", "fact_spare", "w3_bf16", "w1_bf16", "fact_spare")
-JOIN_TAGS = ("w3_raw", "w4_raw", "w3_raw", "w4_raw", "w3_raw")
-FACT_ON_VECTOR = (0,0,0,0,0,0)
-FUSED = (0,0,0,0,0,0)
+SHOP_FACTOR = 0.7
 FLOPS = 2 * K * H * S * 3 + 2 * H * N * U
+
+SPARE = 16
+CHUNK = 256
+SHOP_PIECES = (512, 256, 128, 128)
+TAIL = 256
+SHOP_PLANES_ON_VECTOR = 1
+W1_GROUPS_ON_SCALAR = 24
 
 
 def tile_picked_ystarjn_sum_p_kernel(
@@ -35,19 +38,12 @@ def tile_picked_ystarjn_sum_p_kernel(
     with ExitStack() as ctx:
         keep = ctx.enter_context(tc.tile_pool(name="keep", bufs=1))
         ring = ctx.enter_context(tc.tile_pool(name="ring", bufs=3))
-        banks = ctx.enter_context(tc.psum_pool(name="banks", bufs=4))
-        out_banks = ctx.enter_context(tc.psum_pool(name="out_banks", bufs=4))
+        banks = ctx.enter_context(tc.psum_pool(name="banks", bufs=PACK))
+        out_banks = ctx.enter_context(tc.psum_pool(name="out_banks", bufs=PACK))
 
         def load_list(src, name):
             tile = keep.tile(list(src.shape), U16, name=name)
             nc.sync.dma_start(tile[:], src)
-            return tile
-
-        def load_scales(src, name, clearer, queue):
-            tile = keep.tile([P, T], U8, name=name, align_bytes=64)
-            clearer.memset(tile[:].bitcast(I32), 0)
-            for r in range(4):
-                queue.dma_start(tile[r:P:32, :].bitcast(I32), src[0, r:16:4, :].bitcast(I32))
             return tile
 
         def load_words(src, name):
@@ -55,70 +51,71 @@ def tile_picked_ystarjn_sum_p_kernel(
             nc.sync.dma_start(tile[:].bitcast(I32), src[0].rearrange("p c r -> p (c r)").bitcast(I32))
             return tile
 
-        def load_weight(src, name):
-            tile = keep.tile([P, PACK, src.shape[1]], F32, name=name, tag=name)
-            nc.sync.dma_start(tile[:], src.rearrange("(p j) c -> p j c", j=PACK))
+        def load_scales(src, name):
+            tile = keep.tile([P, T], U8, name=name, align_bytes=64)
+            nc.vector.memset(tile[:].bitcast(I32), 0)
+            for r in range(PACK):
+                nc.sync.dma_start(tile[r:P:QUADRANT, :].bitcast(I32), src[0, r:K // BLOCK:PACK, :].bitcast(I32))
             return tile
 
+        def load_weight(src, name):
+            raw = keep.tile([P, PACK, src.shape[1]], F32, name=name, tag=name)
+            nc.sync.dma_start(raw[:], src.rearrange("(p j) c -> p j c", j=PACK))
+            return raw
+
         def pick(words, scales, picks, name):
-            got_words = keep.tile([P, S], U32, name=name + "_words_picked", align_bytes=64)
-            nc.vector.tensor_copy(got_words[:], words[:].indirect(picks[:]))
-            got_scales = keep.tile([P, S], U8, name=name + "_scales_picked", align_bytes=64)
-            nc.vector.tensor_copy(got_scales[:], scales[:].indirect(picks[:]))
-            return got_words, got_scales
-
-        def quantize(rounded, width, name):
-            codes = keep.tile([P, width], U32, name=name + "_codes", align_bytes=64)
-            scales = keep.tile([P, width], U8, name=name + "_scales", align_bytes=64)
-            nc.vector.quantize_mx(out=codes[:].bitcast(FP8X4), scales=scales[:], in_=rounded)
-            return codes, scales
-
-        def quantize_planes(rounded, width, name):
-            codes = keep.tile([P, width], U32, name=name + "_codes", align_bytes=64)
-            scales = keep.tile([P, width], U8, name=name + "_scales", align_bytes=64)
-            for a, b in ((0, 128), (128, 512)):
-                nc.vector.quantize_mx(
-                    out=codes[:, a:b].bitcast(FP8X4), scales=scales[:, a:b], in_=rounded[:, PACK * a:PACK * b])
-            return codes, scales
+            picked_words = keep.tile([P, S], U32, name=name + "_words_picked", align_bytes=64)
+            nc.vector.tensor_copy(picked_words[:], words[:].indirect(picks[:]))
+            picked_scales = keep.tile([P, S], U8, name=name + "_scales_picked", align_bytes=64)
+            nc.vector.tensor_copy(picked_scales[:], scales[:].indirect(picks[:]))
+            return picked_words, picked_scales
 
         def round_dealt(parts, name):
             rounded = keep.tile([P, PACK, P, PACK], BF16, name=name + "_bf16", tag=name + "_bf16", align_bytes=64)
             dst = rounded[:].rearrange("p (a b) m j -> p a m j b", a=2)
-            m0 = 0
-            for raw, on_scalar, on_gpsimd in parts:
+            first = 0
+            for raw, on_scalar in parts:
                 src = raw[:].rearrange("p j (m a b) -> p a m j b", a=2, b=2)
-                width = src.shape[2]
+                groups = src.shape[2]
                 if on_scalar > 0:
                     for a in range(2):
-                        nc.scalar.activation(dst[:, a, m0:m0 + on_scalar], src[:, a, :on_scalar], COPY)
-                rest = width - on_gpsimd
-                if on_scalar < rest:
-                    nc.vector.tensor_copy(dst[:, :, m0 + on_scalar:m0 + rest], src[:, :, on_scalar:rest])
-                if on_gpsimd > 0:
-                    nc.gpsimd.tensor_scalar(dst[:, m0 + rest:m0 + width], src[:, rest:], 1.0, 0.0, MULT, ADD)
-                m0 = m0 + width
+                        nc.scalar.activation(dst[:, a, first:first + on_scalar], src[:, a, :on_scalar], COPY)
+                if on_scalar < groups:
+                    nc.vector.tensor_copy(dst[:, :, first + on_scalar:first + groups], src[:, :, on_scalar:])
+                first = first + groups
             return rounded[:].rearrange("p t m j -> p (t m j)")
 
-        def product(w_codes, w_scales, got_words, got_scales, factor, name):
-            rows = []
+        def quantize(rounded, cuts, name):
+            codes = keep.tile([P, cuts[-1]], U32, name=name + "_codes", align_bytes=64)
+            scales = keep.tile([P, cuts[-1]], U8, name=name + "_scales", align_bytes=64)
+            for a, b in zip(cuts, cuts[1:]):
+                nc.vector.quantize_mx(
+                    out=codes[:, a:b].bitcast(FP8X4), scales=scales[:, a:b], in_=rounded[:, PACK * a:PACK * b])
+            return codes, scales
+
+        def multiply(acc, weight, block, moving):
+            cols = slice(block * P, (block + 1) * P)
+            nc.tensor.matmul_mx(
+                out=acc, lhsT=weight[0][:, cols].bitcast(FP8X4), lhsT_scale=weight[1][:, cols],
+                rhs=moving[0][:].bitcast(FP8X4), rhs_scale=moving[1][:], start=True, stop=True,
+            )
+
+        def product(weight, picked, factor, offsets, name):
+            planes = []
             for t in range(PACK):
                 bank = banks.tile([P, S], F32, name="bank")
-                cols = slice(t * P, (t + 1) * P)
-                nc.tensor.matmul_mx(
-                    out=bank[:], lhsT=w_codes[:, cols].bitcast(FP8X4), lhsT_scale=w_scales[:, cols],
-                    rhs=got_words[:].bitcast(FP8X4), rhs_scale=got_scales[:], start=True, stop=True,
-                )
-                row = keep.tile([P, S], F32, name=name + str(t))
+                multiply(bank[:], weight, t, picked)
+                plane = keep.tile([P, max(S, offsets + SPARE)], F32, name=name + str(t))
                 if factor is None:
-                    nc.scalar.copy(row[:], bank[:])
+                    nc.scalar.copy(plane[:, :S], bank[:])
                 else:
-                    nc.scalar.activation(row[:], bank[:], COPY, scale=factor[:, t:t + 1])
-                rows.append(row)
-            return rows
+                    nc.scalar.activation(plane[:, :S], bank[:], COPY, scale=factor[:, t:t + 1])
+                planes.append(plane)
+            return planes
 
         x_word_rows = load_words(x_words, "x_word_rows")
         offs_sb = load_list(offs, "offs_sb")
-        x_scale_rows = load_scales(x_scales, "x_scale_rows", nc.vector, nc.sync)
+        x_scale_rows = load_scales(x_scales, "x_scale_rows")
         w1_low = load_weight(w1[:, :H // 2], "w1_low")
         w1_high = load_weight(w1[:, H // 2:], "w1_high")
         unit_sb = keep.tile([P, PACK], F32, name="unit_sb")
@@ -126,10 +123,10 @@ def tile_picked_ystarjn_sum_p_kernel(
         e_word_rows = load_words(e_words, "e_word_rows")
         fk_sb = load_list(fk, "fk_sb")
         prd_sb = load_list(prd, "prd_sb")
-        e_scale_rows = load_scales(e_scales, "e_scale_rows", nc.vector, nc.sync)
+        e_scale_rows = load_scales(e_scales, "e_scale_rows")
         d_word_rows = load_words(d_words, "d_word_rows")
         shp_sb = load_list(shp, "shp_sb")
-        d_scale_rows = load_scales(d_scales, "d_scale_rows", nc.vector, nc.sync)
+        d_scale_rows = load_scales(d_scales, "d_scale_rows")
         w2_raw = load_weight(w2, "w2_raw")
         dk1_sb = load_list(dk1, "dk1_sb")
         w3_raw = load_weight(w3, "w3_raw")
@@ -137,124 +134,71 @@ def tile_picked_ystarjn_sum_p_kernel(
         w4_raw = load_weight(w4, "w4_raw")
 
         shop_unit = keep.tile([P, PACK], F32, name="shop_unit")
+        nc.scalar.activation(shop_unit[:], unit_sb[:], COPY, scale=SHOP_FACTOR)
 
-        nc.scalar.activation(shop_unit[:], unit_sb[:], COPY, scale=0.7)
-        x_got = pick(x_word_rows, x_scale_rows, offs_sb, "x")
-        w1_q = quantize_planes(round_dealt([(w1_low, 64, 0), (w1_high, 24, 0)], "w1"), H, "w1")
-        fact = product(*w1_q, *x_got, unit_sb, "fact")
-        e_got = pick(e_word_rows, e_scale_rows, prd_sb, "e")
-        d_got = pick(d_word_rows, d_scale_rows, shp_sb, "d")
-        w2_q = quantize(round_dealt([(w2_raw, 0, 0)], "w2"), H, "w2")
-        goods = product(*w2_q, *e_got, None, "goods")
-        w3_q = quantize(round_dealt([(w3_raw, 0, 0)], "w3"), H, "w3")
-        shop = product(*w3_q, *d_got, shop_unit, "shop")
+        x_picked = pick(x_word_rows, x_scale_rows, offs_sb, "x")
+        w1_q = quantize(round_dealt([(w1_low, P // 2), (w1_high, W1_GROUPS_ON_SCALAR)], "w1"), (0, P, H), "w1")
+        fact = product(w1_q, x_picked, unit_sb, U, "fact")
+        e_picked = pick(e_word_rows, e_scale_rows, prd_sb, "e")
+        d_picked = pick(d_word_rows, d_scale_rows, shp_sb, "d")
+        w2_q = quantize(round_dealt([(w2_raw, 0)], "w2"), (0, H), "w2")
+        goods = product(w2_q, e_picked, None, U, "goods")
+        w3_q = quantize(round_dealt([(w3_raw, 0)], "w3"), (0, H), "w3")
+        shop = product(w3_q, d_picked, shop_unit, max(SHOP_PIECES), "shop")
 
         w4_bf16 = keep.tile([P, N, PACK], BF16, name="w4_bf16", align_bytes=64)
         nc.vector.tensor_copy(
             w4_bf16[:].rearrange("p (c i) j -> p c j i", i=2), w4_raw[:].rearrange("p j (c i) -> p c j i", i=2))
-        w4_codes, w4_scales = quantize(w4_bf16[:].rearrange("p c j -> p (c j)"), N, "w4")
+        w4_q = quantize(w4_bf16[:].rearrange("p c j -> p (c j)"), (0, N), "w4")
 
-        starts = [sum(CHUNKS[:c]) for c in range(len(CHUNKS))]
-        piece_starts = [sum(PIECES[:c]) for c in range(len(PIECES))]
-        fact_parts, joined_parts, shop_parts = {}, {}, {}
+        joined = keep.tile([P, PACK, U], F32, name="joined", tag="w3_raw")
+        for pair, tag in enumerate(("w1_bf16", "w3_bf16")):
+            facts = keep.tile([P, 2, U], F32, name="facts", tag=tag, align_bytes=64)
+            for b in range(2):
+                nc.scalar.activation(facts[:, b, :], fact[2 * pair + b][:].indirect(fk_sb[:]), COPY)
+            for b in range(2):
+                t = 2 * pair + b
+                nc.vector.tensor_tensor(joined[:, t, :], goods[t][:].indirect(dk1_sb[:]), facts[:, b, :], MULT)
 
-        def entries(start, n):
-            return slice(start // 16, (start + n) // 16)
+        def quantized_hid(start, width, shops):
+            hid = ring.tile([P, width, PACK], BF16, name="hid", align_bytes=64)
+            nc.vector.tensor_tensor(
+                hid[:].rearrange("p (c i) t -> p c t i", i=2),
+                joined[:, :, start:start + width].rearrange("p t (c i) -> p c t i", i=2),
+                shops.rearrange("p t (c i) -> p c t i", i=2), ADD)
+            return quantize(hid[:].rearrange("p r t -> p (r t)"), (0, width), "hid" + str(start))
 
-        def fetch_facts(h, planes):
-            if h not in fact_parts:
-                fact_parts[h] = keep.tile(
-                    [P, PACK, PIECES[h]], F32, name="fact_part", tag=FACT_TAGS[h], align_bytes=64)
-            for t in planes:
-                picked = fact[t][:].indirect(fk_sb[:, entries(piece_starts[h], PIECES[h])])
-                if t >= PACK - FACT_ON_VECTOR[h]:
-                    nc.vector.tensor_copy(fact_parts[h][:, t, :], picked)
-                else:
-                    nc.scalar.activation(fact_parts[h][:, t, :], picked, COPY)
-
-        def times_goods(h, planes):
-            if h not in joined_parts:
-                joined_parts[h] = keep.tile([P, PACK, PIECES[h]], F32, name="joined", tag=JOIN_TAGS[h])
-            for t in planes:
-                nc.vector.tensor_tensor(
-                    joined_parts[h][:, t, :], goods[t][:].indirect(dk1_sb[:, entries(piece_starts[h], PIECES[h])]),
-                    fact_parts[h][:, t, :], MULT)
-
-        def fetch_shops(c):
-            shop_parts[c] = ring.tile([P, PACK, CHUNKS[c]], F32, name="shop_part")
-            h = max(k for k in range(len(PIECES)) if piece_starts[k] <= starts[c])
-            inside = starts[c] - piece_starts[h]
+        tail_start = U - TAIL
+        tail_banks = [banks.tile([P, TAIL], F32, name="bank") for block in range(N // P)]
+        piece_start = 0
+        for piece in SHOP_PIECES:
+            entries = dk2_sb[:, piece_start // LIST_ROWS:(piece_start + piece) // LIST_ROWS]
+            shops = ring.tile([P, PACK, piece], F32, name="shops")
             for t in range(PACK):
-                picked = shop[t][:].indirect(dk2_sb[:, entries(starts[c], CHUNKS[c])])
-                if FUSED[c]:
-                    nc.vector.tensor_tensor(
-                        shop_parts[c][:, t, :], picked, joined_parts[h][:, t, inside:inside + CHUNKS[c]], ADD)
-                elif t < SHOP_ON_VECTOR[c]:
-                    nc.vector.tensor_copy(shop_parts[c][:, t, :], picked)
+                if piece_start == 0 and t < SHOP_PLANES_ON_VECTOR:
+                    nc.vector.tensor_copy(shops[:, t, :], shop[t][:].indirect(entries))
                 else:
-                    nc.scalar.activation(shop_parts[c][:, t, :], picked, COPY)
+                    nc.scalar.activation(shops[:, t, :], shop[t][:].indirect(entries), COPY)
 
-        def finish(c):
-            n = CHUNKS[c]
-            h = max(k for k in range(len(PIECES)) if piece_starts[k] <= starts[c])
-            inside = starts[c] - piece_starts[h]
-            hid = ring.tile([P, n, PACK], BF16, name="hid", align_bytes=64)
-            woven = hid[:].rearrange("p (c i) t -> p c t i", i=2)
-            shop_woven = shop_parts[c][:].rearrange("p t (c i) -> p c t i", i=2)
-            if FUSED[c] == 1:
-                nc.vector.tensor_copy(woven, shop_woven)
-            elif FUSED[c] == 2:
-                nc.scalar.copy(woven, shop_woven)
-            else:
-                nc.vector.tensor_tensor(
-                    woven, joined_parts[h][:, :, inside:inside + n].rearrange("p t (c i) -> p c t i", i=2), shop_woven, ADD)
-            hid_codes, hid_scales = quantize(hid[:].rearrange("p r t -> p (r t)"), n, "hid" + str(c))
-            cols_out = slice(starts[c], starts[c] + n)
-            if OUT_ON_SCALAR[c] == 2:
-                for b in range(N // P):
-                    cols = slice(b * P, (b + 1) * P)
-                    acc = out_banks.tile([P, n], F32, name="acc")
-                    nc.tensor.matmul_mx(
-                        out=acc[:], lhsT=w4_codes[:, cols].bitcast(FP8X4), lhsT_scale=w4_scales[:, cols],
-                        rhs=hid_codes[:].bitcast(FP8X4), rhs_scale=hid_scales[:], start=True, stop=True,
-                    )
-                    result = ring.tile([P, n], F32, name="last_result")
-                    if b == 0:
-                        nc.scalar.copy(result[:], acc[:])
-                        nc.scalar.dma_start(out[cols, cols_out], result[:])
-                    else:
-                        nc.vector.tensor_copy(result[:], acc[:])
-                        nc.sync.dma_start(out[cols, cols_out], result[:])
-                return
-            acc = out_banks.tile([P, N // P, n], F32, name="acc")
-            for b in range(N // P):
-                cols = slice(b * P, (b + 1) * P)
-                nc.tensor.matmul_mx(
-                    out=acc[:, b, :], lhsT=w4_codes[:, cols].bitcast(FP8X4), lhsT_scale=w4_scales[:, cols],
-                    rhs=hid_codes[:].bitcast(FP8X4), rhs_scale=hid_scales[:], start=True, stop=True,
-                )
-            result = ring.tile([P, N // P, n], F32, name="result")
-            if OUT_ON_SCALAR[c]:
-                nc.scalar.copy(result[:], acc[:])
-            else:
-                nc.vector.tensor_copy(result[:], acc[:])
-            nc.sync.dma_start(out[:, cols_out].rearrange("(b p) r -> p b r", p=P), result[:])
+            width = min(piece, CHUNK)
+            for inside in range(0, piece, width):
+                start = piece_start + inside
+                hid_q = quantized_hid(start, width, shops[:, :, inside:inside + width])
+                if start >= tail_start:
+                    for block in range(N // P):
+                        multiply(tail_banks[block][:, start - tail_start:start - tail_start + width], w4_q, block, hid_q)
+                else:
+                    acc = out_banks.tile([P, N // P, width], F32, name="acc")
+                    for block in range(N // P):
+                        multiply(acc[:, block, :], w4_q, block, hid_q)
+                    result = ring.tile([P, N // P, width], F32, name="result")
+                    nc.scalar.copy(result[:], acc[:])
+                    nc.sync.dma_start(out[:, start:start + width].rearrange("(b p) r -> p b r", p=P), result[:])
+            piece_start = piece_start + piece
 
-        fetch_facts(0, [0,1,2,3])
-        fetch_facts(1, [0,1,2,3])
-        times_goods(0, [0,1,2,3])
-        fetch_shops(0)
-        fetch_facts(2, [0,1,2,3])
-        times_goods(1, [0,1,2,3])
-        finish(0)
-        fetch_shops(1)
-        fetch_facts(3, [0,1,2,3])
-        times_goods(2, [0,1,2,3])
-        finish(1)
-        fetch_shops(2)
-        times_goods(3, [0,1,2,3])
-        finish(2)
-        fetch_shops(3)
-        fetch_shops(4)
-        finish(3)
-        finish(4)
+        tail_low = keep.tile([P, TAIL], F32, name="tail_low")
+        nc.scalar.copy(tail_low[:], tail_banks[0][:])
+        nc.scalar.dma_start(out[:P, tail_start:], tail_low[:])
+        tail_high = keep.tile([P, TAIL], F32, name="tail_high")
+        nc.vector.tensor_copy(tail_high[:], tail_banks[1][:])
+        nc.sync.dma_start(out[P:, tail_start:], tail_high[:])

@@ -93,8 +93,8 @@ def tile_picked_ystarjn_sum_p_kernel(
                     out=codes[:, a:b].bitcast(FP8X4), scales=scales[:, a:b], in_=rounded[:, PACK * a:PACK * b])
             return codes, scales
 
-        def multiply(acc, weight, block, moving):
-            cols = slice(block * P, (block + 1) * P)
+        def multiply(acc, weight, slab, moving):
+            cols = slice(slab * P, (slab + 1) * P)
             nc.tensor.matmul_mx(
                 out=acc, lhsT=weight[0][:, cols].bitcast(FP8X4), lhsT_scale=weight[1][:, cols],
                 rhs=moving[0][:].bitcast(FP8X4), rhs_scale=moving[1][:], start=True, stop=True,
@@ -118,31 +118,30 @@ def tile_picked_ystarjn_sum_p_kernel(
         x_scale_rows = load_scales(x_scales, "x_scale_rows")
         w1_low = load_weight(w1[:, :H // 2], "w1_low")
         w1_high = load_weight(w1[:, H // 2:], "w1_high")
-        unit_sb = keep.tile([P, PACK], F32, name="unit_sb")
-        nc.sync.dma_start(unit_sb[:], unit.rearrange("(p t) o -> p (t o)", t=PACK))
         e_word_rows = load_words(e_words, "e_word_rows")
-        fk_sb = load_list(fk, "fk_sb")
-        prd_sb = load_list(prd, "prd_sb")
         e_scale_rows = load_scales(e_scales, "e_scale_rows")
+        prd_sb = load_list(prd, "prd_sb")
         d_word_rows = load_words(d_words, "d_word_rows")
         shp_sb = load_list(shp, "shp_sb")
+        fk_sb = load_list(fk, "fk_sb")
         d_scale_rows = load_scales(d_scales, "d_scale_rows")
         w2_raw = load_weight(w2, "w2_raw")
-        dk1_sb = load_list(dk1, "dk1_sb")
+        unit_sb = keep.tile([P, PACK], F32, name="unit_sb")
+        nc.sync.dma_start(unit_sb[:], unit.rearrange("(p t) o -> p (t o)", t=PACK))
         w3_raw = load_weight(w3, "w3_raw")
-        dk2_sb = load_list(dk2, "dk2_sb")
+        dk1_sb = load_list(dk1, "dk1_sb")
         w4_raw = load_weight(w4, "w4_raw")
-
-        shop_unit = keep.tile([P, PACK], F32, name="shop_unit")
-        nc.scalar.activation(shop_unit[:], unit_sb[:], COPY, scale=SHOP_FACTOR)
+        dk2_sb = load_list(dk2, "dk2_sb")
 
         x_picked = pick(x_word_rows, x_scale_rows, offs_sb, "x")
         w1_q = quantize(round_dealt([(w1_low, P // 2), (w1_high, W1_GROUPS_ON_SCALAR)], "w1"), (0, P, H), "w1")
-        fact = product(w1_q, x_picked, unit_sb, U, "fact")
+        fact = product(w1_q, x_picked, None, U, "fact")
         e_picked = pick(e_word_rows, e_scale_rows, prd_sb, "e")
         d_picked = pick(d_word_rows, d_scale_rows, shp_sb, "d")
         w2_q = quantize(round_dealt([(w2_raw, 0)], "w2"), (0, H), "w2")
-        goods = product(w2_q, e_picked, None, U, "goods")
+        shop_unit = keep.tile([P, PACK], F32, name="shop_unit")
+        nc.scalar.activation(shop_unit[:], unit_sb[:], COPY, scale=SHOP_FACTOR)
+        goods = product(w2_q, e_picked, unit_sb, U, "goods")
         w3_q = quantize(round_dealt([(w3_raw, 0)], "w3"), (0, H), "w3")
         shop = product(w3_q, d_picked, shop_unit, max(SHOP_PIECES), "shop")
 
@@ -169,7 +168,7 @@ def tile_picked_ystarjn_sum_p_kernel(
             return quantize(hid[:].rearrange("p r t -> p (r t)"), (0, width), "hid" + str(start))
 
         tail_start = U - TAIL
-        tail_banks = [banks.tile([P, TAIL], F32, name="bank") for block in range(N // P)]
+        tail_banks = [banks.tile([P, TAIL], F32, name="bank") for slab in range(N // P)]
         piece_start = 0
         for piece in SHOP_PIECES:
             entries = dk2_sb[:, piece_start // LIST_ROWS:(piece_start + piece) // LIST_ROWS]
@@ -185,12 +184,12 @@ def tile_picked_ystarjn_sum_p_kernel(
                 start = piece_start + inside
                 hid_q = quantized_hid(start, width, shops[:, :, inside:inside + width])
                 if start >= tail_start:
-                    for block in range(N // P):
-                        multiply(tail_banks[block][:, start - tail_start:start - tail_start + width], w4_q, block, hid_q)
+                    for slab in range(N // P):
+                        multiply(tail_banks[slab][:, start - tail_start:start - tail_start + width], w4_q, slab, hid_q)
                 else:
                     acc = out_banks.tile([P, N // P, width], F32, name="acc")
-                    for block in range(N // P):
-                        multiply(acc[:, block, :], w4_q, block, hid_q)
+                    for slab in range(N // P):
+                        multiply(acc[:, slab, :], w4_q, slab, hid_q)
                     result = ring.tile([P, N // P, width], F32, name="result")
                     nc.scalar.copy(result[:], acc[:])
                     nc.sync.dma_start(out[:, start:start + width].rearrange("(b p) r -> p b r", p=P), result[:])

from contextlib import ExitStack

import concourse.mybir as mybir

F32 = mybir.dt.float32
BF16 = mybir.dt.bfloat16
I32 = mybir.dt.int32
U32 = mybir.dt.uint32
U16 = mybir.dt.uint16
U8 = mybir.dt.uint8
FP8X4 = mybir.dt.float8_e4m3fn_x4
MULT = mybir.AluOpType.mult
ADD = mybir.AluOpType.add
COPY = mybir.ActivationFunctionType.Copy

P = 128
PACK = 4
LIST_ROWS = 16
BLOCK = 32
QUADRANT = 32
K, T, S, H, N, U = 512, 1024, 512, 512, 256, 1024
SHOP_FACTOR = 0.7
FLOPS = 2 * K * H * S * 3 + 2 * H * N * U

SPARE = 16
CHUNK = 256
SHOP_PIECES = (512, 256, 128, 128)
TAIL = 256
SHOP_PLANES_ON_VECTOR = 1
W1_GROUPS_ON_SCALAR = 24


def tile_picked_ystarjn_sum_p_kernel(
    tc, x_words, x_scales, w1, e_words, e_scales, w2, d_words, d_scales, w3, unit, w4,
    offs, prd, shp, fk, dk1, dk2, out,
):
    nc = tc.nc
    with ExitStack() as ctx:
        keep = ctx.enter_context(tc.tile_pool(name="keep", bufs=1))
        ring = ctx.enter_context(tc.tile_pool(name="ring", bufs=3))
        banks = ctx.enter_context(tc.psum_pool(name="banks", bufs=PACK))
        out_banks = ctx.enter_context(tc.psum_pool(name="out_banks", bufs=PACK))

        def load_list(src, name):
            tile = keep.tile(list(src.shape), U16, name=name)
            nc.sync.dma_start(tile[:], src)
            return tile

        def load_words(src, name):
            tile = keep.tile([P, T], U32, name=name, align_bytes=64)
            nc.sync.dma_start(tile[:].bitcast(I32), src[0].rearrange("p c r -> p (c r)").bitcast(I32))
            return tile

        def load_scales(src, name):
            tile = keep.tile([P, T], U8, name=name, align_bytes=64)
            nc.vector.memset(tile[:].bitcast(I32), 0)
            for r in range(PACK):
                nc.sync.dma_start(tile[r:P:QUADRANT, :].bitcast(I32), src[0, r:K // BLOCK:PACK, :].bitcast(I32))
            return tile

        def load_weight(src, name):
            raw = keep.tile([P, PACK, src.shape[1]], F32, name=name, tag=name)
            nc.sync.dma_start(raw[:], src.rearrange("(p j) c -> p j c", j=PACK))
            return raw

        def pick(words, scales, picks, name):
            picked_words = keep.tile([P, S], U32, name=name + "_words_picked", align_bytes=64)
            nc.vector.tensor_copy(picked_words[:], words[:].indirect(picks[:]))
            picked_scales = keep.tile([P, S], U8, name=name + "_scales_picked", align_bytes=64)
            nc.vector.tensor_copy(picked_scales[:], scales[:].indirect(picks[:]))
            return picked_words, picked_scales

        def round_dealt(parts, name):
            rounded = keep.tile([P, PACK, P, PACK], BF16, name=name + "_bf16", tag=name + "_bf16", align_bytes=64)
            dst = rounded[:].rearrange("p (a b) m j -> p a m j b", a=2)
            first = 0
            for raw, on_scalar in parts:
                src = raw[:].rearrange("p j (m a b) -> p a m j b", a=2, b=2)
                groups = src.shape[2]
                if on_scalar > 0:
                    for a in range(2):
                        nc.scalar.activation(dst[:, a, first:first + on_scalar], src[:, a, :on_scalar], COPY)
                if on_scalar < groups:
                    nc.vector.tensor_copy(dst[:, :, first + on_scalar:first + groups], src[:, :, on_scalar:])
                first = first + groups
            return rounded[:].rearrange("p t m j -> p (t m j)")

        def quantize(rounded, cuts, name):
            codes = keep.tile([P, cuts[-1]], U32, name=name + "_codes", align_bytes=64)
            scales = keep.tile([P, cuts[-1]], U8, name=name + "_scales", align_bytes=64)
            for a, b in zip(cuts, cuts[1:]):
                nc.vector.quantize_mx(
                    out=codes[:, a:b].bitcast(FP8X4), scales=scales[:, a:b], in_=rounded[:, PACK * a:PACK * b])
            return codes, scales

        def multiply(acc, weight, slab, moving):
            cols = slice(slab * P, (slab + 1) * P)
            nc.tensor.matmul_mx(
                out=acc, lhsT=weight[0][:, cols].bitcast(FP8X4), lhsT_scale=weight[1][:, cols],
                rhs=moving[0][:].bitcast(FP8X4), rhs_scale=moving[1][:], start=True, stop=True,
            )

        def product(weight, picked, factor, offsets, name):
            planes = []
            for t in range(PACK):
                bank = banks.tile([P, S], F32, name="bank")
                multiply(bank[:], weight, t, picked)
                plane = keep.tile([P, max(S, offsets + SPARE)], F32, name=name + str(t))
                if factor is None:
                    nc.scalar.copy(plane[:, :S], bank[:])
                else:
                    nc.scalar.activation(plane[:, :S], bank[:], COPY, scale=factor[:, t:t + 1])
                planes.append(plane)
            return planes

        x_word_rows = load_words(x_words, "x_word_rows")
        offs_sb = load_list(offs, "offs_sb")
        x_scale_rows = load_scales(x_scales, "x_scale_rows")
        w1_low = load_weight(w1[:, :H // 2], "w1_low")
        w1_high = load_weight(w1[:, H // 2:], "w1_high")
        e_word_rows = load_words(e_words, "e_word_rows")
        e_scale_rows = load_scales(e_scales, "e_scale_rows")
        prd_sb = load_list(prd, "prd_sb")
        d_word_rows = load_words(d_words, "d_word_rows")
        shp_sb = load_list(shp, "shp_sb")
        fk_sb = load_list(fk, "fk_sb")
        d_scale_rows = load_scales(d_scales, "d_scale_rows")
        w2_raw = load_weight(w2, "w2_raw")
        unit_sb = keep.tile([P, PACK], F32, name="unit_sb")
        nc.sync.dma_start(unit_sb[:], unit.rearrange("(p t) o -> p (t o)", t=PACK))
        w3_raw = load_weight(w3, "w3_raw")
        dk1_sb = load_list(dk1, "dk1_sb")
        w4_raw = load_weight(w4, "w4_raw")
        dk2_sb = load_list(dk2, "dk2_sb")

        x_picked = pick(x_word_rows, x_scale_rows, offs_sb, "x")
        w1_q = quantize(round_dealt([(w1_low, P // 2), (w1_high, W1_GROUPS_ON_SCALAR)], "w1"), (0, P, H), "w1")
        fact = product(w1_q, x_picked, None, U, "fact")
        e_picked = pick(e_word_rows, e_scale_rows, prd_sb, "e")
        d_picked = pick(d_word_rows, d_scale_rows, shp_sb, "d")
        w2_q = quantize(round_dealt([(w2_raw, 0)], "w2"), (0, H), "w2")
        shop_unit = keep.tile([P, PACK], F32, name="shop_unit")
        nc.scalar.activation(shop_unit[:], unit_sb[:], COPY, scale=SHOP_FACTOR)
        goods = product(w2_q, e_picked, unit_sb, U, "goods")
        w3_q = quantize(round_dealt([(w3_raw, 0)], "w3"), (0, H), "w3")
        shop = product(w3_q, d_picked, shop_unit, max(SHOP_PIECES), "shop")

        w4_bf16 = keep.tile([P, N, PACK], BF16, name="w4_bf16", align_bytes=64)
        nc.vector.tensor_copy(
            w4_bf16[:].rearrange("p (c i) j -> p c j i", i=2), w4_raw[:].rearrange("p j (c i) -> p c j i", i=2))
        w4_q = quantize(w4_bf16[:].rearrange("p c j -> p (c j)"), (0, N), "w4")

        joined = keep.tile([P, PACK, U], F32, name="joined", tag="w3_raw")
        for pair, tag in enumerate(("w1_bf16", "w3_bf16")):
            facts = keep.tile([P, 2, U], F32, name="facts", tag=tag, align_bytes=64)
            for b in range(2):
                nc.scalar.activation(facts[:, b, :], fact[2 * pair + b][:].indirect(fk_sb[:]), COPY)
            for b in range(2):
                t = 2 * pair + b
                nc.vector.tensor_tensor(joined[:, t, :], goods[t][:].indirect(dk1_sb[:]), facts[:, b, :], MULT)

        def quantized_hid(start, width, shops):
            hid = ring.tile([P, width, PACK], BF16, name="hid", align_bytes=64)
            nc.vector.tensor_tensor(
                hid[:].rearrange("p (c i) t -> p c t i", i=2),
                joined[:, :, start:start + width].rearrange("p t (c i) -> p c t i", i=2),
                shops.rearrange("p t (c i) -> p c t i", i=2), ADD)
            return quantize(hid[:].rearrange("p r t -> p (r t)"), (0, width), "hid" + str(start))

        tail_start = U - TAIL
        tail_banks = [banks.tile([P, TAIL], F32, name="bank") for slab in range(N // P)]
        piece_start = 0
        for piece in SHOP_PIECES:
            entries = dk2_sb[:, piece_start // LIST_ROWS:(piece_start + piece) // LIST_ROWS]
            shops = ring.tile([P, PACK, piece], F32, name="shops")
            for t in range(PACK):
                if piece_start == 0 and t < SHOP_PLANES_ON_VECTOR:
                    nc.vector.tensor_copy(shops[:, t, :], shop[t][:].indirect(entries))
                else:
                    nc.scalar.activation(shops[:, t, :], shop[t][:].indirect(entries), COPY)

            width = min(piece, CHUNK)
            for inside in range(0, piece, width):
                start = piece_start + inside
                hid_q = quantized_hid(start, width, shops[:, :, inside:inside + width])
                if start >= tail_start:
                    for slab in range(N // P):
                        multiply(tail_banks[slab][:, start - tail_start:start - tail_start + width], w4_q, slab, hid_q)
                else:
                    acc = out_banks.tile([P, N // P, width], F32, name="acc")
                    for slab in range(N // P):
                        multiply(acc[:, slab, :], w4_q, slab, hid_q)
                    result = ring.tile([P, N // P, width], F32, name="result")
                    nc.scalar.copy(result[:], acc[:])
                    nc.sync.dma_start(out[:, start:start + width].rearrange("(b p) r -> p b r", p=P), result[:])
            piece_start = piece_start + piece

        tail_low = keep.tile([P, TAIL], F32, name="tail_low")
        nc.scalar.copy(tail_low[:], tail_banks[0][:])
        nc.scalar.dma_start(out[:P, tail_start:], tail_low[:])
        tail_high = keep.tile([P, TAIL], F32, name="tail_high")
        nc.vector.tensor_copy(tail_high[:], tail_banks[1][:])
        nc.sync.dma_start(out[P:, tail_start:], tail_high[:])
